import numpy as np
import ml_dtypes


def mxq(x, axis, fmt="e4m3"):
    dtype, down = {"e4m3": (ml_dtypes.float8_e4m3fn, 7), "e5m2": (ml_dtypes.float8_e5m2, 14)}[fmt]
    v = np.moveaxis(np.asarray(x, np.float32).astype(ml_dtypes.bfloat16).astype(np.float64), axis, -1)
    blocks = v.reshape(v.shape[:-1] + (-1, 32))
    amax = np.abs(blocks).max(-1, keepdims=True)
    byte = np.maximum(np.where(amax > 0, np.frexp(amax)[1] - 1 + 127, 0) - down, 1)
    scale = np.exp2(byte - 127.0)
    codes = (blocks / scale).astype(np.float32).astype(dtype).astype(np.float64)
    return np.moveaxis((codes * scale).reshape(v.shape), -1, axis)


WIDE = False


def mx_kscale(k):
    if not WIDE:
        return np.ones(k)
    levels = np.array([10, -10, 5, -5, 0])
    if k % 512:
        return np.exp2(np.random.permutation(np.resize(levels, k // 32))).repeat(32)
    a = np.empty((k // 512, 16))
    for p in range(k // 512):
        a[p, :8] = np.random.permutation(np.resize(levels, 8))
        for g in range(8):
            far = levels[np.abs(levels - a[p, g]) >= 10]
            a[p, g + 8] = far[np.random.randint(len(far))]
    return np.exp2(a.ravel()).repeat(32)


def f64(x):
    return np.asarray(x).astype(np.float64)


E2M1 = np.array([0.0, 0.5, 1.0, 1.5, 2.0, 3.0, 4.0, 6.0, -0.0, -0.5, -1.0, -1.5, -2.0, -3.0, -4.0, -6.0])


def pack_weight(w, fmt):
    k, n = w.shape
    w = f64(np.asarray(w, np.float32).astype(ml_dtypes.bfloat16)).reshape(k // 32, 32, n)
    amax = np.abs(w).max(1)
    if fmt == "e4m3":
        byte = np.frexp(amax)[1] - 1 + 127 - 7
    else:
        mant, ex = np.frexp(amax / 6.0)
        byte = np.where(mant > 0.5, ex, ex - 1) + 127
    byte = np.clip(np.where(amax > 0, byte, 1), 1, 254)
    scaled = (w * np.exp2(127.0 - byte)[:, None, :]).reshape(k, n).astype(np.float32)
    by_word = np.ascontiguousarray(scaled.reshape(k // 512, 128, 4, n).transpose(0, 1, 3, 2))
    if fmt == "e4m3":
        words = by_word.astype(ml_dtypes.float8_e4m3fn).view(np.uint8)
    else:
        c = by_word.astype(ml_dtypes.float4_e2m1fn).view(np.uint8) & 0xF
        words = (c[..., 0::2] | (c[..., 1::2] << 4)).reshape(k // 512, 128, 2 * n)
    return np.ascontiguousarray(words), np.ascontiguousarray(byte.astype(np.uint8).reshape(k // 512, 16, n))


def unpack_weight(words, scales, fmt):
    g, _, n = scales.shape
    words = np.ascontiguousarray(words).reshape(g, 128, n, -1)
    if fmt == "e4m3":
        vals = words.view(ml_dtypes.float8_e4m3fn).astype(np.float64)
    else:
        nib = np.empty((g, 128, n, 4), np.uint8)
        nib[..., 0::2] = words & 0xF
        nib[..., 1::2] = words >> 4
        vals = E2M1[nib]
    vals = vals * np.repeat(np.exp2(scales.astype(np.float64) - 127.0), 8, axis=1)[..., None]
    return vals.transpose(0, 1, 3, 2).reshape(g * 512, n)


def gelu(v):
    return 0.5 * v * (1.0 + np.tanh(np.sqrt(2.0 / np.pi) * (v + 0.044715 * v**3)))


O, K, M, T = 512, 1536, 512, 1024


def setup_inputs():
    n = np.random.standard_normal
    s = mx_kscale(K)[:, None]
    x = n((K, T)); x[:O] *= 6.0
    w = n((K, M)) / np.sqrt(K) / s; w[:O] /= 2.0
    p_x4 = pack_weight(x[O:] * s[O:], "e2m1")
    p_w4 = pack_weight(w[O:], "e2m1")
    return {
        "x8": (x[:O] * s[:O]).astype(np.float32),
        "w8": (w[:O]).astype(np.float32),
        "x4_words": p_x4[0],
        "x4_scales": p_x4[1],
        "w4_words": p_w4[0],
        "w4_scales": p_w4[1],
        "b": (0.3 * n(512)).astype(np.float32),
    }


def reference(x8, w8, x4_words, x4_scales, w4_words, w4_scales, b):
    x8_ = mxq(f64(x8), 0, "e4m3")
    w8_ = mxq(f64(w8), 0, "e4m3")
    x4_ = unpack_weight(x4_words, x4_scales, "e2m1")
    w4_ = unpack_weight(w4_words, w4_scales, "e2m1")
    y = w8_.T @ x8_ + w4_.T @ x4_
    return gelu(y + f64(b)[:, None])

@@ -1,0 +1,189 @@
+from contextlib import ExitStack
+
+import concourse.mybir as mybir
+from concourse.masks import make_identity
+
+F32 = mybir.dt.float32
+BF16 = mybir.dt.bfloat16
+I32 = mybir.dt.int32
+U32 = mybir.dt.uint32
+U8 = mybir.dt.uint8
+E4M3 = mybir.dt.float8_e4m3fn_x4
+E2M1 = mybir.dt.float4_e2m1fn_x4
+GELU = mybir.ActivationFunctionType.Gelu_apprx_tanh
+
+P = 128
+K8, K4, N_OUT, T = 512, 1024, 512, 1024
+A = K4 // 512
+MT = N_OUT // P
+TQ = 256
+Q = T // TQ
+SUB = 128
+
+FLOPS = 2 * (K8 + K4) * N_OUT * T
+
+
+def tile_mix_atom_fm_gelu_kernel(tc, x8, w8, x4_words, x4_scales, w4_words, w4_scales, b, out):
+    nc = tc.nc
+    x8_v = x8.rearrange("(p j) t -> p j t", j=4)
+    w8_v = w8.rearrange("(p j) n -> p j n", j=4)
+    x4_v = x4_words.rearrange("a p c -> p a c")
+    w4_v = w4_words.rearrange("a p c -> p a c")
+    out_v = out.rearrange("(m p) t -> p m t", p=P)
+
+    with ExitStack() as ctx:
+        keep = ctx.enter_context(tc.tile_pool(name="keep", bufs=1))
+        stage = ctx.enter_context(tc.tile_pool(name="stage", bufs=1))
+        psum = ctx.enter_context(tc.psum_pool(name="psum", bufs=8))
+        ctx.enter_context(tc.manual_schedule())
+
+        w4 = keep.tile([P, A, 2 * N_OUT], U8, align_bytes=64)
+        x4a = keep.tile([P, A, T], U8, align_bytes=64)
+        x4b = keep.tile([P, A, T], U8, align_bytes=64)
+        w4s = keep.tile([P, A, N_OUT], U8, align_bytes=64)
+        x4s = keep.tile([P, A, T], U8, align_bytes=64)
+        w8c = keep.tile([P, N_OUT], U32, align_bytes=64)
+        w8s = keep.tile([P, N_OUT], U8, align_bytes=64)
+        x8c = keep.tile([P, T], U32, align_bytes=64)
+        x8s = keep.tile([P, T], U8, align_bytes=64)
+        b_rows = keep.tile([P, P], F32)
+        b_cols = keep.tile([P, MT], F32)
+        ident = keep.tile([P, P], F32)
+        warm = keep.tile([P, 8], F32)
+        warm_out = keep.tile([P, 8], F32)
+
+        def load_w8(h):
+            raw = stage.tile([P, 4, 256], F32, tag="raw_w", bufs=2, name="raw_w")
+            nc.sync.dma_start(out=raw[:], in_=w8_v[:, :, 256 * h : 256 * (h + 1)])
+            return raw
+
+        def load_x8(q):
+            raw = stage.tile([P, 4, TQ], F32, tag="raw_x", bufs=4, name="raw_x")
+            nc.sync.dma_start(out=raw[:], in_=x8_v[:, :, TQ * q : TQ * (q + 1)])
+            return raw
+
+        def regroup(raw, s, engine):
+            grouped = stage.tile([P, SUB, 4], BF16, tag="grouped", bufs=12, align_bytes=64, name="grouped")
+            src = raw[:, :, SUB * s : SUB * (s + 1)].rearrange("p j w -> p w j")
+            if engine == "scalar":
+                nc.scalar.copy(out=grouped[:], in_=src)
+            else:
+                nc.vector.tensor_copy(out=grouped[:], in_=src)
+            return grouped
+
+        def quantise(grouped, codes, scales):
+            nc.vector.quantize_mx(
+                out=codes.bitcast(E4M3),
+                scales=scales,
+                in_=grouped[:].rearrange("p w j -> p (w j)"),
+            )
+
+        nc.vector.memset(x4s[:].rearrange("p a n -> p (a n)").bitcast(I32), 0)
+        nc.vector.memset(w4s[:].rearrange("p a n -> p (a n)").bitcast(I32), 0)
+        nc.vector.memset(b_rows[:], 0.0)
+        nc.vector.memset(warm[:], 0.0)
+
+        nc.sync.dma_start(out=w4[:], in_=w4_v)
+        nc.sync.dma_start(out=x4a[:], in_=x4_v[:, :, 0:T])
+        for r in range(4):
+            nc.scalar.dma_start(
+                out=w4s[32 * r : 32 * r + 4, :, :].bitcast(I32),
+                in_=w4_scales[:, 4 * r : 4 * r + 4, :].rearrange("a r n -> r a n").bitcast(I32),
+            )
+            nc.gpsimd.dma_start(
+                out=x4s[32 * r : 32 * r + 4, :, :].bitcast(I32),
+                in_=x4_scales[:, 4 * r : 4 * r + 4, :].rearrange("a r n -> r a n").bitcast(I32),
+            )
+        make_identity(nc, ident[:])
+        nc.scalar.activation(out=warm_out[:], in_=warm[:], func=GELU)
+
+        raw_w = [None, None]
+        raw_x = [None, None, None, None]
+        raw_w[0] = load_w8(0)
+        raw_x[0] = load_x8(0)
+        nc.sync.dma_start(out=b_rows[0:MT, :], in_=b.rearrange("(m p) -> m p", p=P))
+        raw_w[1] = load_w8(1)
+        raw_x[1] = load_x8(1)
+        nc.sync.dma_start(out=x4b[:], in_=x4_v[:, :, T : 2 * T])
+        raw_x[2] = load_x8(2)
+        raw_x[3] = load_x8(3)
+
+        acc = {}
+
+        def e2m1_passes(q):
+            x4_half = x4a if q < 2 else x4b
+            c0 = 2 * TQ * (q % 2)
+            for m in range(MT):
+                bank = psum.tile([P, 512], F32, tag="bank", bufs=8, name="bank")
+                acc[q, m] = bank
+                for a in range(A):
+                    nc.tensor.matmul_mx(
+                        out=bank[:, 0:TQ],
+                        lhsT=w4[:, a, 2 * P * m : 2 * P * (m + 1)].bitcast(E2M1),
+                        lhsT_scale=w4s[:, a, P * m : P * (m + 1)],
+                        rhs=x4_half[:, a, c0 : c0 + 2 * TQ].bitcast(E2M1),
+                        rhs_scale=x4s[:, a, TQ * q : TQ * (q + 1)],
+                        start=(a == 0),
+                        stop=False,
+                    )
+
+        def e4m3_passes(q, ms):
+            for m in ms:
+                nc.tensor.matmul_mx(
+                    out=acc[q, m][:, 0:TQ],
+                    lhsT=w8c[:, P * m : P * (m + 1)].bitcast(E4M3),
+                    lhsT_scale=w8s[:, P * m : P * (m + 1)],
+                    rhs=x8c[:, TQ * q : TQ * (q + 1)].bitcast(E4M3),
+                    rhs_scale=x8s[:, TQ * q : TQ * (q + 1)],
+                    start=False,
+                    stop=True,
+                )
+
+        def finish(q, ms):
+            o = stage.tile([P, 2, TQ], F32, tag="o", bufs=8, name="o")
+            for i, m in enumerate(ms):
+                nc.scalar.activation(
+                    out=o[:, i, :], in_=acc[q, m][:, 0:TQ], func=GELU, bias=b_cols[:, m : m + 1]
+                )
+            nc.sync.dma_start(
+                out=out_v[:, ms[0] : ms[0] + len(ms), TQ * q : TQ * (q + 1)], in_=o[:, 0 : len(ms), :]
+            )
+
+        def prep_w8(h, engines):
+            g = [regroup(raw_w[h], s, engines[s]) for s in range(2)]
+            for s in range(2):
+                c = slice(256 * h + SUB * s, 256 * h + SUB * (s + 1))
+                quantise(g[s], w8c[:, c], w8s[:, c])
+
+        def prep_x8(q, engines):
+            g = [regroup(raw_x[q], s, engines[s]) for s in range(2)]
+            for s in range(2):
+                c = slice(TQ * q + SUB * s, TQ * q + SUB * (s + 1))
+                quantise(g[s], x8c[:, c], x8s[:, c])
+
+        bias_ps = psum.tile([P, 512], F32, tag="bank", bufs=8, name="bias_ps")
+        e2m1_passes(0)
+        nc.tensor.transpose(bias_ps[:, 0:P], b_rows[:], ident[:])
+        prep_w8(0, ("vector", "scalar"))
+        e2m1_passes(1)
+        prep_x8(0, ("vector", "vector"))
+        nc.vector.tensor_copy(out=b_cols[:], in_=bias_ps[:, 0:MT])
+        e4m3_passes(0, (0, 1))
+        finish(0, (0, 1))
+        prep_w8(1, ("vector", "vector"))
+        e4m3_passes(0, (2, 3))
+        finish(0, (2, 3))
+        prep_x8(1, ("vector", "vector"))
+        e2m1_passes(2)
+        e4m3_passes(1, (0, 1, 2, 3))
+        finish(1, (0, 1))
+        finish(1, (2, 3))
+        prep_x8(2, ("vector", "vector"))
+        e2m1_passes(3)
+        e4m3_passes(2, (0, 1, 2, 3))
+        finish(2, (0, 1))
+        finish(2, (2, 3))
+        prep_x8(3, ("vector", "vector"))
+        e4m3_passes(3, (0, 1, 2, 3))
+        finish(3, (0, 1))
+        finish(3, (2, 3))

@@ -38,8 +38,7 @@ def tile_mix_atom_fm_gelu_kernel(tc, x8, w8, x4_words, x4_scales, w4_words, w4_s
         ctx.enter_context(tc.manual_schedule())
 
         w4 = keep.tile([P, A, 2 * N_OUT], U8, align_bytes=64)
-        x4a = keep.tile([P, A, T], U8, align_bytes=64)
-        x4b = keep.tile([P, A, T], U8, align_bytes=64)
+        x4 = keep.tile([P, A, 2 * T], U8, align_bytes=64)
         w4s = keep.tile([P, A, N_OUT], U8, align_bytes=64)
         x4s = keep.tile([P, A, T], U8, align_bytes=64)
         w8c = keep.tile([P, N_OUT], U32, align_bytes=64)
@@ -78,13 +77,14 @@ def tile_mix_atom_fm_gelu_kernel(tc, x8, w8, x4_words, x4_scales, w4_words, w4_s
                 in_=grouped[:].rearrange("p w j -> p (w j)"),
             )
 
+        nc.vector.memset(b_rows[:], 0.0)
         nc.vector.memset(x4s[:].rearrange("p a n -> p (a n)").bitcast(I32), 0)
         nc.vector.memset(w4s[:].rearrange("p a n -> p (a n)").bitcast(I32), 0)
-        nc.vector.memset(b_rows[:], 0.0)
         nc.vector.memset(warm[:], 0.0)
 
         nc.sync.dma_start(out=w4[:], in_=w4_v)
-        nc.sync.dma_start(out=x4a[:], in_=x4_v[:, :, 0:T])
+        nc.sync.dma_start(out=x4[:], in_=x4_v)
+        nc.scalar.dma_start(out=b_rows[0:MT, :], in_=b.rearrange("(m p) -> m p", p=P))
         for r in range(4):
             nc.scalar.dma_start(
                 out=w4s[32 * r : 32 * r + 4, :, :].bitcast(I32),
@@ -101,19 +101,15 @@ def tile_mix_atom_fm_gelu_kernel(tc, x8, w8, x4_words, x4_scales, w4_words, w4_s
         raw_x = [None, None, None, None]
         raw_w[0] = load_w8(0)
         raw_x[0] = load_x8(0)
-        nc.sync.dma_start(out=b_rows[0:MT, :], in_=b.rearrange("(m p) -> m p", p=P))
         raw_w[1] = load_w8(1)
         raw_x[1] = load_x8(1)
-        nc.sync.dma_start(out=x4b[:], in_=x4_v[:, :, T : 2 * T])
         raw_x[2] = load_x8(2)
         raw_x[3] = load_x8(3)
 
         acc = {}
 
-        def e2m1_passes(q):
-            x4_half = x4a if q < 2 else x4b
-            c0 = 2 * TQ * (q % 2)
-            for m in range(MT):
+        def e2m1_passes(q, ms):
+            for m in ms:
                 bank = psum.tile([P, 512], F32, tag="bank", bufs=8, name="bank")
                 acc[q, m] = bank
                 for a in range(A):
@@ -121,7 +117,7 @@ def tile_mix_atom_fm_gelu_kernel(tc, x8, w8, x4_words, x4_scales, w4_words, w4_s
                         out=bank[:, 0:TQ],
                         lhsT=w4[:, a, 2 * P * m : 2 * P * (m + 1)].bitcast(E2M1),
                         lhsT_scale=w4s[:, a, P * m : P * (m + 1)],
-                        rhs=x4_half[:, a, c0 : c0 + 2 * TQ].bitcast(E2M1),
+                        rhs=x4[:, a, 2 * TQ * q : 2 * TQ * (q + 1)].bitcast(E2M1),
                         rhs_scale=x4s[:, a, TQ * q : TQ * (q + 1)],
                         start=(a == 0),
                         stop=False,
@@ -162,28 +158,17 @@ def tile_mix_atom_fm_gelu_kernel(tc, x8, w8, x4_words, x4_scales, w4_words, w4_s
                 quantise(g[s], x8c[:, c], x8s[:, c])
 
         bias_ps = psum.tile([P, 512], F32, tag="bank", bufs=8, name="bias_ps")
-        e2m1_passes(0)
         nc.tensor.transpose(bias_ps[:, 0:P], b_rows[:], ident[:])
         prep_w8(0, ("vector", "scalar"))
-        e2m1_passes(1)
-        prep_x8(0, ("vector", "vector"))
         nc.vector.tensor_copy(out=b_cols[:], in_=bias_ps[:, 0:MT])
-        e4m3_passes(0, (0, 1))
-        finish(0, (0, 1))
-        prep_w8(1, ("vector", "vector"))
-        e4m3_passes(0, (2, 3))
-        finish(0, (2, 3))
-        prep_x8(1, ("vector", "vector"))
-        e2m1_passes(2)
-        e4m3_passes(1, (0, 1, 2, 3))
-        finish(1, (0, 1))
-        finish(1, (2, 3))
-        prep_x8(2, ("vector", "vector"))
-        e2m1_passes(3)
-        e4m3_passes(2, (0, 1, 2, 3))
-        finish(2, (0, 1))
-        finish(2, (2, 3))
-        prep_x8(3, ("vector", "vector"))
-        e4m3_passes(3, (0, 1, 2, 3))
-        finish(3, (0, 1))
-        finish(3, (2, 3))
+        for q in range(Q):
+            if q == Q - 1:
+                e2m1_passes(q, (0, 1, 2, 3))
+            prep_x8(q, ("vector", "vector"))
+            if q == 0:
+                prep_w8(1, ("vector", "vector"))
+            for ms in ((0, 1), (2, 3)):
+                if q < Q - 1:
+                    e2m1_passes(q, ms)
+                e4m3_passes(q, ms)
+                finish(q, ms)

@@ -51,9 +51,9 @@ def tile_mix_atom_fm_gelu_kernel(tc, x8, w8, x4_words, x4_scales, w4_words, w4_s
         warm = keep.tile([P, 8], F32)
         warm_out = keep.tile([P, 8], F32)
 
-        def load_w8(h):
+        def load_w8(engine, h):
             raw = stage.tile([P, 4, 256], F32, tag="raw_w", bufs=2, name="raw_w")
-            nc.sync.dma_start(out=raw[:], in_=w8_v[:, :, 256 * h : 256 * (h + 1)])
+            engine.dma_start(out=raw[:], in_=w8_v[:, :, 256 * h : 256 * (h + 1)])
             return raw
 
         def load_x8(q):
@@ -77,34 +77,32 @@ def tile_mix_atom_fm_gelu_kernel(tc, x8, w8, x4_words, x4_scales, w4_words, w4_s
                 in_=grouped[:].rearrange("p w j -> p (w j)"),
             )
 
-        nc.vector.memset(b_rows[:], 0.0)
         nc.vector.memset(x4s[:].rearrange("p a n -> p (a n)").bitcast(I32), 0)
         nc.vector.memset(w4s[:].rearrange("p a n -> p (a n)").bitcast(I32), 0)
         nc.vector.memset(warm[:], 0.0)
+        nc.vector.memset(b_rows[:], 0.0)
 
-        nc.sync.dma_start(out=w4[:], in_=w4_v)
-        nc.sync.dma_start(out=x4[:], in_=x4_v)
-        nc.scalar.dma_start(out=b_rows[0:MT, :], in_=b.rearrange("(m p) -> m p", p=P))
-        for r in range(4):
-            nc.scalar.dma_start(
-                out=w4s[32 * r : 32 * r + 4, :, :].bitcast(I32),
-                in_=w4_scales[:, 4 * r : 4 * r + 4, :].rearrange("a r n -> r a n").bitcast(I32),
+        def load_scales(engine, plane, src, r):
+            engine.dma_start(
+                out=plane[32 * r : 32 * r + 4, :, :].bitcast(I32),
+                in_=src[:, 4 * r : 4 * r + 4, :].rearrange("a r n -> r a n").bitcast(I32),
             )
-            nc.gpsimd.dma_start(
-                out=x4s[32 * r : 32 * r + 4, :, :].bitcast(I32),
-                in_=x4_scales[:, 4 * r : 4 * r + 4, :].rearrange("a r n -> r a n").bitcast(I32),
-            )
-        make_identity(nc, ident[:])
-        nc.scalar.activation(out=warm_out[:], in_=warm[:], func=GELU)
 
         raw_w = [None, None]
         raw_x = [None, None, None, None]
-        raw_w[0] = load_w8(0)
+        nc.gpsimd.dma_start(out=w4[:].bitcast(I32), in_=w4_v.bitcast(I32))
+        nc.gpsimd.dma_start(out=x4[:].bitcast(I32), in_=x4_v.bitcast(I32))
+        raw_w[0] = load_w8(nc.gpsimd, 0)
+        make_identity(nc, ident[:])
+        for r in range(4):
+            load_scales(nc.sync, x4s, x4_scales, r)
+            load_scales(nc.scalar, w4s, w4_scales, r)
+        nc.scalar.activation(out=warm_out[:], in_=warm[:], func=GELU)
+        nc.scalar.dma_start(out=b_rows[0:MT, :], in_=b.rearrange("(m p) -> m p", p=P))
         raw_x[0] = load_x8(0)
-        raw_w[1] = load_w8(1)
-        raw_x[1] = load_x8(1)
-        raw_x[2] = load_x8(2)
-        raw_x[3] = load_x8(3)
+        raw_w[1] = load_w8(nc.sync, 1)
+        for q in range(1, Q):
+            raw_x[q] = load_x8(q)
 
         acc = {}
 
@@ -158,17 +156,21 @@ def tile_mix_atom_fm_gelu_kernel(tc, x8, w8, x4_words, x4_scales, w4_words, w4_s
                 quantise(g[s], x8c[:, c], x8s[:, c])
 
         bias_ps = psum.tile([P, 512], F32, tag="bank", bufs=8, name="bias_ps")
-        nc.tensor.transpose(bias_ps[:, 0:P], b_rows[:], ident[:])
+        e2m1_passes(0, (0, 1, 2, 3))
         prep_w8(0, ("vector", "scalar"))
+        prep_x8(0, ("vector", "vector"))
+        nc.tensor.transpose(bias_ps[:, 0:P], b_rows[:], ident[:])
         nc.vector.tensor_copy(out=b_cols[:], in_=bias_ps[:, 0:MT])
-        for q in range(Q):
-            if q == Q - 1:
-                e2m1_passes(q, (0, 1, 2, 3))
+        e4m3_passes(0, (0, 1))
+        finish(0, (0, 1))
+        e2m1_passes(1, (0, 1, 2, 3))
+        prep_w8(1, ("vector", "vector"))
+        e4m3_passes(0, (2, 3))
+        finish(0, (2, 3))
+        for q in range(1, Q):
             prep_x8(q, ("vector", "vector"))
-            if q == 0:
-                prep_w8(1, ("vector", "vector"))
             for ms in ((0, 1), (2, 3)):
-                if q < Q - 1:
-                    e2m1_passes(q, ms)
                 e4m3_passes(q, ms)
                 finish(q, ms)
+            if q + 1 < Q:
+                e2m1_passes(q + 1, (0, 1, 2, 3))

@@ -51,9 +51,9 @@ def tile_mix_atom_fm_gelu_kernel(tc, x8, w8, x4_words, x4_scales, w4_words, w4_s
         warm = keep.tile([P, 8], F32)
         warm_out = keep.tile([P, 8], F32)
 
-        def load_w8(engine, h):
+        def load_w8(h):
             raw = stage.tile([P, 4, 256], F32, tag="raw_w", bufs=2, name="raw_w")
-            engine.dma_start(out=raw[:], in_=w8_v[:, :, 256 * h : 256 * (h + 1)])
+            nc.sync.dma_start(out=raw[:], in_=w8_v[:, :, 256 * h : 256 * (h + 1)])
             return raw
 
         def load_x8(q):
@@ -77,10 +77,11 @@ def tile_mix_atom_fm_gelu_kernel(tc, x8, w8, x4_words, x4_scales, w4_words, w4_s
                 in_=grouped[:].rearrange("p w j -> p (w j)"),
             )
 
+        nc.gpsimd.memset(w4s[:].rearrange("p a n -> p (a n)").bitcast(I32), 0)
         nc.vector.memset(x4s[:].rearrange("p a n -> p (a n)").bitcast(I32), 0)
-        nc.vector.memset(w4s[:].rearrange("p a n -> p (a n)").bitcast(I32), 0)
         nc.vector.memset(warm[:], 0.0)
-        nc.vector.memset(b_rows[:], 0.0)
+        nc.gpsimd.memset(b_rows[:], 0.0)
+        make_identity(nc, ident[:])
 
         def load_scales(engine, plane, src, r):
             engine.dma_start(
@@ -90,17 +91,20 @@ def tile_mix_atom_fm_gelu_kernel(tc, x8, w8, x4_words, x4_scales, w4_words, w4_s
 
         raw_w = [None, None]
         raw_x = [None, None, None, None]
-        nc.gpsimd.dma_start(out=w4[:].bitcast(I32), in_=w4_v.bitcast(I32))
-        nc.gpsimd.dma_start(out=x4[:].bitcast(I32), in_=x4_v.bitcast(I32))
-        raw_w[0] = load_w8(nc.gpsimd, 0)
-        make_identity(nc, ident[:])
-        for r in range(4):
-            load_scales(nc.sync, x4s, x4_scales, r)
-            load_scales(nc.scalar, w4s, w4_scales, r)
-        nc.scalar.activation(out=warm_out[:], in_=warm[:], func=GELU)
-        nc.scalar.dma_start(out=b_rows[0:MT, :], in_=b.rearrange("(m p) -> m p", p=P))
+        nc.sync.dma_start(out=w4[:], in_=w4_v)
+        load_scales(nc.sync, w4s, w4_scales, 0)
+        load_scales(nc.sync, w4s, w4_scales, 1)
+        load_scales(nc.scalar, w4s, w4_scales, 2)
+        load_scales(nc.scalar, w4s, w4_scales, 3)
+        load_scales(nc.scalar, x4s, x4_scales, 0)
+        nc.sync.dma_start(out=x4[:], in_=x4_v)
+        raw_w[0] = load_w8(0)
         raw_x[0] = load_x8(0)
-        raw_w[1] = load_w8(nc.sync, 1)
+        for r in range(1, 4):
+            load_scales(nc.scalar, x4s, x4_scales, r)
+        nc.scalar.dma_start(out=b_rows[0:MT, :], in_=b.rearrange("(m p) -> m p", p=P))
+        nc.scalar.activation(out=warm_out[:], in_=warm[:], func=GELU)
+        raw_w[1] = load_w8(1)
         for q in range(1, Q):
             raw_x[q] = load_x8(q)
 
@@ -156,21 +160,22 @@ def tile_mix_atom_fm_gelu_kernel(tc, x8, w8, x4_words, x4_scales, w4_words, w4_s
                 quantise(g[s], x8c[:, c], x8s[:, c])
 
         bias_ps = psum.tile([P, 512], F32, tag="bank", bufs=8, name="bias_ps")
-        e2m1_passes(0, (0, 1, 2, 3))
         prep_w8(0, ("vector", "scalar"))
         prep_x8(0, ("vector", "vector"))
+        e2m1_passes(0, (0, 1))
         nc.tensor.transpose(bias_ps[:, 0:P], b_rows[:], ident[:])
         nc.vector.tensor_copy(out=b_cols[:], in_=bias_ps[:, 0:MT])
         e4m3_passes(0, (0, 1))
         finish(0, (0, 1))
-        e2m1_passes(1, (0, 1, 2, 3))
+        e2m1_passes(0, (2, 3))
+        e2m1_passes(1, (0, 1))
         prep_w8(1, ("vector", "vector"))
         e4m3_passes(0, (2, 3))
         finish(0, (2, 3))
         for q in range(1, Q):
             prep_x8(q, ("vector", "vector"))
             for ms in ((0, 1), (2, 3)):
+                if (q, ms) != (1, (0, 1)):
+                    e2m1_passes(q, ms)
                 e4m3_passes(q, ms)
                 finish(q, ms)
-            if q + 1 < Q:
-                e2m1_passes(q + 1, (0, 1, 2, 3))

from contextlib import ExitStack

import concourse.mybir as mybir
from concourse.masks import make_identity

F32 = mybir.dt.float32
BF16 = mybir.dt.bfloat16
I32 = mybir.dt.int32
U32 = mybir.dt.uint32
U8 = mybir.dt.uint8
E4M3 = mybir.dt.float8_e4m3fn_x4
E2M1 = mybir.dt.float4_e2m1fn_x4
GELU = mybir.ActivationFunctionType.Gelu_apprx_tanh

P = 128
K8, K4, N_OUT, T = 512, 1024, 512, 1024
A = K4 // 512
MT = N_OUT // P
TQ = 256
Q = T // TQ
SUB = 128

FLOPS = 2 * (K8 + K4) * N_OUT * T


def tile_mix_atom_fm_gelu_kernel(tc, x8, w8, x4_words, x4_scales, w4_words, w4_scales, b, out):
    nc = tc.nc
    x8_v = x8.rearrange("(p j) t -> p j t", j=4)
    w8_v = w8.rearrange("(p j) n -> p j n", j=4)
    x4_v = x4_words.rearrange("a p c -> p a c")
    w4_v = w4_words.rearrange("a p c -> p a c")
    out_v = out.rearrange("(m p) t -> p m t", p=P)

    with ExitStack() as ctx:
        keep = ctx.enter_context(tc.tile_pool(name="keep", bufs=1))
        stage = ctx.enter_context(tc.tile_pool(name="stage", bufs=1))
        psum = ctx.enter_context(tc.psum_pool(name="psum", bufs=8))
        ctx.enter_context(tc.manual_schedule())

        w4 = keep.tile([P, A, 2 * N_OUT], U8, align_bytes=64)
        x4 = keep.tile([P, A, 2 * T], U8, align_bytes=64)
        w4s = keep.tile([P, A, N_OUT], U8, align_bytes=64)
        x4s = keep.tile([P, A, T], U8, align_bytes=64)
        w8c = keep.tile([P, N_OUT], U32, align_bytes=64)
        w8s = keep.tile([P, N_OUT], U8, align_bytes=64)
        x8c = keep.tile([P, T], U32, align_bytes=64)
        x8s = keep.tile([P, T], U8, align_bytes=64)
        b_rows = keep.tile([P, P], F32)
        b_cols = keep.tile([P, MT], F32)
        ident = keep.tile([P, P], F32)
        warm = keep.tile([P, 8], F32)
        warm_out = keep.tile([P, 8], F32)

        def load_w8(h):
            raw = stage.tile([P, 4, 256], F32, tag="raw_w", bufs=2, name="raw_w")
            nc.sync.dma_start(out=raw[:], in_=w8_v[:, :, 256 * h : 256 * (h + 1)])
            return raw

        def load_x8(q):
            raw = stage.tile([P, 4, TQ], F32, tag="raw_x", bufs=4, name="raw_x")
            nc.sync.dma_start(out=raw[:], in_=x8_v[:, :, TQ * q : TQ * (q + 1)])
            return raw

        def regroup(raw, s, engine):
            grouped = stage.tile([P, SUB, 4], BF16, tag="grouped", bufs=12, align_bytes=64, name="grouped")
            src = raw[:, :, SUB * s : SUB * (s + 1)].rearrange("p j w -> p w j")
            if engine == "scalar":
                nc.scalar.copy(out=grouped[:], in_=src)
            else:
                nc.vector.tensor_copy(out=grouped[:], in_=src)
            return grouped

        def quantise(grouped, codes, scales):
            nc.vector.quantize_mx(
                out=codes.bitcast(E4M3),
                scales=scales,
                in_=grouped[:].rearrange("p w j -> p (w j)"),
            )

        nc.gpsimd.memset(w4s[:].rearrange("p a n -> p (a n)").bitcast(I32), 0)
        nc.vector.memset(x4s[:].rearrange("p a n -> p (a n)").bitcast(I32), 0)
        nc.vector.memset(warm[:], 0.0)
        nc.gpsimd.memset(b_rows[:], 0.0)
        make_identity(nc, ident[:])

        def load_scales(engine, plane, src, r):
            engine.dma_start(
                out=plane[32 * r : 32 * r + 4, :, :].bitcast(I32),
                in_=src[:, 4 * r : 4 * r + 4, :].rearrange("a r n -> r a n").bitcast(I32),
            )

        raw_w = [None, None]
        raw_x = [None, None, None, None]
        nc.sync.dma_start(out=w4[:], in_=w4_v)
        load_scales(nc.sync, w4s, w4_scales, 0)
        load_scales(nc.sync, w4s, w4_scales, 1)
        load_scales(nc.scalar, w4s, w4_scales, 2)
        load_scales(nc.scalar, w4s, w4_scales, 3)
        load_scales(nc.scalar, x4s, x4_scales, 0)
        nc.sync.dma_start(out=x4[:], in_=x4_v)
        raw_w[0] = load_w8(0)
        raw_x[0] = load_x8(0)
        for r in range(1, 4):
            load_scales(nc.scalar, x4s, x4_scales, r)
        nc.scalar.dma_start(out=b_rows[0:MT, :], in_=b.rearrange("(m p) -> m p", p=P))
        nc.scalar.activation(out=warm_out[:], in_=warm[:], func=GELU)
        raw_w[1] = load_w8(1)
        for q in range(1, Q):
            raw_x[q] = load_x8(q)

        acc = {}

        def e2m1_passes(q, ms):
            for m in ms:
                bank = psum.tile([P, 512], F32, tag="bank", bufs=8, name="bank")
                acc[q, m] = bank
                for a in range(A):
                    nc.tensor.matmul_mx(
                        out=bank[:, 0:TQ],
                        lhsT=w4[:, a, 2 * P * m : 2 * P * (m + 1)].bitcast(E2M1),
                        lhsT_scale=w4s[:, a, P * m : P * (m + 1)],
                        rhs=x4[:, a, 2 * TQ * q : 2 * TQ * (q + 1)].bitcast(E2M1),
                        rhs_scale=x4s[:, a, TQ * q : TQ * (q + 1)],
                        start=(a == 0),
                        stop=False,
                    )

        def e4m3_passes(q, ms):
            for m in ms:
                nc.tensor.matmul_mx(
                    out=acc[q, m][:, 0:TQ],
                    lhsT=w8c[:, P * m : P * (m + 1)].bitcast(E4M3),
                    lhsT_scale=w8s[:, P * m : P * (m + 1)],
                    rhs=x8c[:, TQ * q : TQ * (q + 1)].bitcast(E4M3),
                    rhs_scale=x8s[:, TQ * q : TQ * (q + 1)],
                    start=False,
                    stop=True,
                )

        def finish(q, ms):
            o = stage.tile([P, 2, TQ], F32, tag="o", bufs=8, name="o")
            for i, m in enumerate(ms):
                nc.scalar.activation(
                    out=o[:, i, :], in_=acc[q, m][:, 0:TQ], func=GELU, bias=b_cols[:, m : m + 1]
                )
            nc.sync.dma_start(
                out=out_v[:, ms[0] : ms[0] + len(ms), TQ * q : TQ * (q + 1)], in_=o[:, 0 : len(ms), :]
            )

        def prep_w8(h, engines):
            g = [regroup(raw_w[h], s, engines[s]) for s in range(2)]
            for s in range(2):
                c = slice(256 * h + SUB * s, 256 * h + SUB * (s + 1))
                quantise(g[s], w8c[:, c], w8s[:, c])

        def prep_x8(q, engines):
            g = [regroup(raw_x[q], s, engines[s]) for s in range(2)]
            for s in range(2):
                c = slice(TQ * q + SUB * s, TQ * q + SUB * (s + 1))
                quantise(g[s], x8c[:, c], x8s[:, c])

        bias_ps = psum.tile([P, 512], F32, tag="bank", bufs=8, name="bias_ps")
        prep_w8(0, ("vector", "scalar"))
        prep_x8(0, ("vector", "vector"))
        e2m1_passes(0, (0, 1))
        nc.tensor.transpose(bias_ps[:, 0:P], b_rows[:], ident[:])
        nc.vector.tensor_copy(out=b_cols[:], in_=bias_ps[:, 0:MT])
        e4m3_passes(0, (0, 1))
        finish(0, (0, 1))
        e2m1_passes(0, (2, 3))
        e2m1_passes(1, (0, 1))
        prep_w8(1, ("vector", "vector"))
        e4m3_passes(0, (2, 3))
        finish(0, (2, 3))
        for q in range(1, Q):
            prep_x8(q, ("vector", "vector"))
            for ms in ((0, 1), (2, 3)):
                if (q, ms) != (1, (0, 1)):
                    e2m1_passes(q, ms)
                e4m3_passes(q, ms)
                finish(q, ms)
